import numpy as np
import ml_dtypes


def mxq(x, axis, fmt="e4m3"):
    dtype, down = {"e4m3": (ml_dtypes.float8_e4m3fn, 7), "e5m2": (ml_dtypes.float8_e5m2, 14)}[fmt]
    v = np.moveaxis(np.asarray(x, np.float32).astype(ml_dtypes.bfloat16).astype(np.float64), axis, -1)
    blocks = v.reshape(v.shape[:-1] + (-1, 32))
    amax = np.abs(blocks).max(-1, keepdims=True)
    byte = np.maximum(np.where(amax > 0, np.frexp(amax)[1] - 1 + 127, 0) - down, 1)
    scale = np.exp2(byte - 127.0)
    codes = (blocks / scale).astype(np.float32).astype(dtype).astype(np.float64)
    return np.moveaxis((codes * scale).reshape(v.shape), -1, axis)


WIDE = False


def mx_kscale(k):
    if not WIDE:
        return np.ones(k)
    levels = np.array([10, -10, 5, -5, 0])
    if k % 512:
        return np.exp2(np.random.permutation(np.resize(levels, k // 32))).repeat(32)
    a = np.empty((k // 512, 16))
    for p in range(k // 512):
        a[p, :8] = np.random.permutation(np.resize(levels, 8))
        for g in range(8):
            far = levels[np.abs(levels - a[p, g]) >= 10]
            a[p, g + 8] = far[np.random.randint(len(far))]
    return np.exp2(a.ravel()).repeat(32)


def f64(x):
    return np.asarray(x).astype(np.float64)


def striped(idx):
    return np.tile(idx.reshape(-1, 16).T, (8, 1)).astype(np.uint16)


def unstriped(offs):
    return offs[:16].T.reshape(-1).astype(np.int64)


def pack_weight(w):
    k, n = w.shape
    w = f64(np.asarray(w, np.float32).astype(ml_dtypes.bfloat16)).reshape(k // 32, 32, n)
    amax = np.abs(w).max(1)
    byte = np.clip(np.where(amax > 0, np.frexp(amax)[1] - 1 + 127 - 7, 1), 1, 254)
    scaled = (w * np.exp2(127.0 - byte)[:, None, :]).reshape(k, n).astype(np.float32)
    words = np.ascontiguousarray(scaled.reshape(k // 512, 128, 4, n).transpose(0, 1, 3, 2)).astype(ml_dtypes.float8_e4m3fn).view(np.uint8)
    return words, np.ascontiguousarray(byte.astype(np.uint8).reshape(k // 512, 16, n))


def unpack_weight(words, scales):
    g, p, n, _ = words.shape
    vals = np.ascontiguousarray(words).view(ml_dtypes.float8_e4m3fn).astype(np.float64) * np.repeat(np.exp2(scales.astype(np.float64) - 127.0), 8, axis=1)[..., None]
    return vals.transpose(0, 1, 3, 2).reshape(g * 512, n)


def sigmoid(v):
    return 1.0 / (1.0 + np.exp(-np.maximum(v, -700.0)))


K, T, S, N, H = 1024, 2048, 512, 256, 512


def setup_inputs():
    n = np.random.standard_normal
    s = mx_kscale(K)[:, None]
    u = mx_kscale(H)
    packed_xT = pack_weight(n((K, T)) * s)
    return {
        "x_words": packed_xT[0],
        "x_scales": packed_xT[1],
        "w1": (n((K, H)) / np.sqrt(K) / s).astype(np.float32),
        "unit": (np.random.uniform(0.6, 1.4, (H, 1)) * u[:, None]).astype(np.float32),
        "w2": (n((H, N)) / np.sqrt(H) / u[:, None]).astype(np.float32),
        "offs": striped(np.random.permutation(T)[:S]),
        "h2": striped(np.random.permutation(S)),
        "h3": striped(np.random.permutation(S)),
    }


def reference(x_words, x_scales, w1, unit, w2, offs, h2, h3):
    xq = unpack_weight(x_words, x_scales)[:, unstriped(offs)]
    y = mxq(f64(w1), 0, "e4m3").T @ xq
    mag = np.abs(y)
    lm = np.log(mag + 0.2)
    l2 = lm[:, unstriped(h2)]
    l3 = lm[:, unstriped(h3)]
    hps = lm + l2 + 0.7 * l3
    m2 = mag[:, unstriped(h2)]
    gm = np.sqrt(mag * m2 + 0.05)
    m3 = mag[:, unstriped(h3)]
    sal = gm - (0.4 * m3)
    hid = f64(unit) * (hps * sigmoid(sal))
    return mxq(f64(w2), 0, "e4m3").T @ mxq(hid, 0, "e4m3")

@@ -1,0 +1,193 @@
+from contextlib import ExitStack
+
+import concourse.mybir as mybir
+
+K, T, S, N, H = 1024, 2048, 512, 256, 512
+FLOPS = 2 * K * H * S + 2 * H * N * S
+
+F32 = mybir.dt.float32
+BF16 = mybir.dt.bfloat16
+I32 = mybir.dt.int32
+U32 = mybir.dt.uint32
+U16 = mybir.dt.uint16
+U8 = mybir.dt.uint8
+FP8X4 = mybir.dt.float8_e4m3fn_x4
+ACT = mybir.ActivationFunctionType
+ALU = mybir.AluOpType
+
+P = 128
+PACK = 4
+K_PASS = P * PACK
+PASSES = K // K_PASS
+WINDOW = 704
+CHUNK = 128
+CHUNKS = S // CHUNK
+THIRD = 0.4
+FLOOR = 0.2 * THIRD
+
+
+def tile_picked_yhpspc_gate_p_kernel(
+    tc, x_words, x_scales, w1, unit, w2, offs, h2, h3, out
+):
+    nc = tc.nc
+    with ExitStack() as ctx:
+        keep = ctx.enter_context(tc.tile_pool(name="keep", bufs=1))
+        psum = ctx.enter_context(tc.psum_pool(name="psum", bufs=1))
+
+        offs_sb = keep.tile([P, S // 16], U16, name="offs_sb")
+        h2_sb = keep.tile([P, S // 16], U16, name="h2_sb")
+        h3_sb = keep.tile([P, S // 16], U16, name="h3_sb")
+        w1_raw = [keep.tile([P, PACK, H], F32, name=f"w1_raw{g}") for g in range(PASSES)]
+        x_all = [keep.tile([P, T], I32, name=f"x_all{g}") for g in range(PASSES)]
+        xs_all = keep.tile([P, T], U8, name="xs_all")
+        w2_raw = keep.tile([P, PACK, N], F32, name="w2_raw")
+        unit_sb = keep.tile([P, PACK], F32, name="unit_sb")
+        mag = [keep.tile([P, WINDOW], F32, name=f"mag{t}") for t in range(PACK)]
+
+        nc.gpsimd.memset(xs_all[:].bitcast(I32), 0)
+        for q in range(4):
+            nc.gpsimd.dma_start(
+                out=xs_all[32 * q : 32 * q + 4 * PASSES, :].bitcast(I32),
+                in_=x_scales[:, 4 * q : 4 * q + 4, :].bitcast(I32),
+            )
+        for t in range(PACK):
+            nc.gpsimd.memset(mag[t][:, S:], 0.0)
+
+        for g in range(PASSES):
+            nc.sync.dma_start(
+                out=w1_raw[g][:],
+                in_=w1[g * K_PASS : (g + 1) * K_PASS, :].rearrange("(p j) c -> p j c", j=PACK),
+            )
+        nc.sync.dma_start(offs_sb[:], offs)
+        for g in range(PASSES):
+            nc.sync.dma_start(
+                out=x_all[g][:], in_=x_words[g].rearrange("p n t -> p (n t)").bitcast(I32)
+            )
+        nc.sync.dma_start(h2_sb[:], h2)
+        nc.sync.dma_start(h3_sb[:], h3)
+        nc.sync.dma_start(out=w2_raw[:], in_=w2.rearrange("(p j) c -> p j c", j=PACK))
+        nc.sync.dma_start(out=unit_sb[:], in_=unit.rearrange("(p t) o -> p (t o)", t=PACK))
+
+        w1_codes = []
+        w1_scales = []
+        for g in range(PASSES):
+            grouped = keep.tile([P, H * PACK], BF16, name=f"w1_grouped{g}", align_bytes=64)
+            dst = grouped[:].rearrange("p (t m r j) -> p m j r t", t=PACK, r=2, j=PACK)
+            src = w1_raw[g][:].rearrange("p j (m r t) -> p m j r t", r=2, t=PACK)
+            if g == 0:
+                nc.scalar.copy(out=dst, in_=src)
+            else:
+                nc.vector.tensor_copy(out=dst, in_=src)
+            codes = keep.tile([P, H], U32, name=f"w1_codes{g}", align_bytes=64)
+            scales = keep.tile([P, H], U8, name=f"w1_scales{g}", align_bytes=64)
+            nc.vector.quantize_mx(out=codes[:].bitcast(FP8X4), scales=scales[:], in_=grouped[:])
+            w1_codes.append(codes)
+            w1_scales.append(scales)
+
+        xs_picked = keep.tile([P, S], U8, name="xs_picked", align_bytes=64)
+        nc.vector.tensor_copy(xs_picked[:], xs_all[:].indirect(offs_sb[:]))
+        y_banks = [psum.tile([P, S], F32, name=f"y{t}") for t in range(PACK)]
+        for g in range(PASSES):
+            x_picked = keep.tile([P, S], U32, name=f"x_picked{g}", align_bytes=64)
+            nc.vector.tensor_copy(x_picked[:], x_all[g][:].bitcast(U32).indirect(offs_sb[:]))
+            for t in range(PACK):
+                cols = slice(t * P, (t + 1) * P)
+                nc.tensor.matmul_mx(
+                    out=y_banks[t][:],
+                    lhsT=w1_codes[g][:, cols].bitcast(FP8X4),
+                    lhsT_scale=w1_scales[g][:, cols],
+                    rhs=x_picked[:].bitcast(FP8X4),
+                    rhs_scale=xs_picked[4 * g :, :],
+                    start=(g == 0),
+                    stop=(g == PASSES - 1),
+                )
+
+        second = keep.tile([P, PACK, S], F32, name="second")
+        second0 = keep.tile([P, S], F32, name="second0")
+        third = keep.tile([P, PACK, S], F32, name="third")
+        prod = keep.tile([P, PACK, S], F32, name="prod")
+        shifted = keep.tile([P, PACK, S], F32, name="shifted")
+        root = keep.tile([P, PACK, S], F32, name="root")
+        hps = keep.tile([P, PACK, S], F32, name="hps")
+
+        for t in range(PACK):
+            nc.scalar.activation(mag[t][:, :S], y_banks[t][:], ACT.Abs, scale=THIRD)
+        for t in range(PACK):
+            if t == 0:
+                nc.vector.tensor_copy(second0[:], mag[t][:].indirect(h2_sb[:]))
+                nc.vector.tensor_scalar_add(second[:, t, :], second0[:], FLOOR)
+            else:
+                nc.scalar.activation(
+                    second[:, t, :], mag[t][:].indirect(h2_sb[:]), ACT.Copy, bias=FLOOR
+                )
+        for t in range(PACK):
+            nc.vector.scalar_tensor_tensor(
+                prod[:, t, :], second[:, t, :], FLOOR, mag[t][:, :S], ALU.subtract, ALU.mult
+            )
+            nc.scalar.activation(
+                root[:, t, :], prod[:, t, :], ACT.Sqrt, bias=0.05, scale=1.0 / THIRD**2
+            )
+            nc.vector.scalar_tensor_tensor(
+                shifted[:, t, :], mag[t][:, :S], FLOOR, second[:, t, :], ALU.add, ALU.mult
+            )
+        for t in range(PACK):
+            nc.vector.tensor_copy(third[:, t, :], mag[t][:].indirect(h3_sb[:]))
+        log12 = prod
+        nc.scalar.activation(log12[:], shifted[:], ACT.Ln, scale=1.0 / THIRD**2)
+        log3 = shifted
+        for t in range(PACK):
+            nc.scalar.activation(log3[:, t, :], third[:, t, :], ACT.Ln, bias=0.2, scale=1.0 / THIRD)
+        for t in range(PACK):
+            nc.vector.tensor_tensor(root[:, t, :], third[:, t, :], root[:, t, :], ALU.subtract)
+        for t in range(PACK):
+            nc.vector.scalar_tensor_tensor(
+                hps[:, t, :], log3[:, t, :], 0.7, log12[:, t, :], ALU.mult, ALU.add
+            )
+
+        w2_grouped = keep.tile([P, N * PACK], BF16, name="w2_grouped", align_bytes=64)
+        nc.vector.tensor_copy(
+            out=w2_grouped[:].rearrange("p (c i j) -> p c j i", i=4, j=PACK),
+            in_=w2_raw[:].rearrange("p j (c i) -> p c j i", i=4),
+        )
+        w2_codes = keep.tile([P, N], U32, name="w2_codes", align_bytes=64)
+        w2_scales = keep.tile([P, N], U8, name="w2_scales", align_bytes=64)
+        nc.vector.quantize_mx(out=w2_codes[:].bitcast(FP8X4), scales=w2_scales[:], in_=w2_grouped[:])
+
+        gate = third
+        for c in range(CHUNKS):
+            cols = slice(c * CHUNK, (c + 1) * CHUNK)
+            nc.scalar.activation(gate[:, :, cols], root[:, :, cols], ACT.Sigmoid, scale=-1.0)
+        out_rows = out.rearrange("(h p) j -> p h j", p=P)
+        for c in range(CHUNKS):
+            cols = slice(c * CHUNK, (c + 1) * CHUNK)
+            hid = keep.tile([P, PACK, CHUNK], BF16, name=f"hid{c}")
+            for t in range(PACK):
+                nc.vector.scalar_tensor_tensor(
+                    hid[:, t, :], hps[:, t, cols], unit_sb[:, t : t + 1], gate[:, t, cols],
+                    ALU.mult, ALU.mult,
+                )
+            hid_grouped = keep.tile([P, CHUNK * PACK], BF16, name=f"hid_grouped{c}", align_bytes=64)
+            nc.vector.tensor_copy(
+                out=hid_grouped[:].rearrange("p (c i t) -> p c t i", i=4, t=PACK),
+                in_=hid[:].rearrange("p t (c i) -> p c t i", i=4),
+            )
+            hid_codes = keep.tile([P, CHUNK], U32, name=f"hid_codes{c}", align_bytes=64)
+            hid_scales = keep.tile([P, CHUNK], U8, name=f"hid_scales{c}", align_bytes=64)
+            nc.vector.quantize_mx(
+                out=hid_codes[:].bitcast(FP8X4), scales=hid_scales[:], in_=hid_grouped[:]
+            )
+            acc = psum.tile([P, N // P, CHUNK], F32, name=f"acc{c}")
+            for h in range(N // P):
+                rows = slice(h * P, (h + 1) * P)
+                nc.tensor.matmul_mx(
+                    out=acc[:, h, :],
+                    lhsT=w2_codes[:, rows].bitcast(FP8X4),
+                    lhsT_scale=w2_scales[:, rows],
+                    rhs=hid_codes[:].bitcast(FP8X4),
+                    rhs_scale=hid_scales[:],
+                    start=True,
+                    stop=True,
+                )
+            result = keep.tile([P, N // P, CHUNK], F32, name=f"result{c}")
+            nc.scalar.copy(out=result[:], in_=acc[:])
+            nc.sync.dma_start(out=out_rows[:, :, cols], in_=result[:])

@@ -51,15 +51,14 @@ def tile_picked_yhpspc_gate_p_kernel(
                 in_=x_scales[:, 4 * q : 4 * q + 4, :].bitcast(I32),
             )
         for t in range(PACK):
-            nc.gpsimd.memset(mag[t][:, S:], 0.0)
+            nc.vector.memset(mag[t][:, S:], 0.0)
+        warm = keep.tile([P, 1], F32, name="warm")
+        nc.scalar.activation(warm[:], mag[0][:, S : S + 1], ACT.Sqrt, bias=0.05)
 
-        for g in range(PASSES):
-            nc.sync.dma_start(
-                out=w1_raw[g][:],
-                in_=w1[g * K_PASS : (g + 1) * K_PASS, :].rearrange("(p j) c -> p j c", j=PACK),
-            )
         nc.sync.dma_start(offs_sb[:], offs)
         for g in range(PASSES):
+            rows = w1[g * K_PASS : (g + 1) * K_PASS, :].rearrange("(p j) c -> p j c", j=PACK)
+            nc.sync.dma_start(out=w1_raw[g][:], in_=rows)
             nc.sync.dma_start(
                 out=x_all[g][:], in_=x_words[g].rearrange("p n t -> p (n t)").bitcast(I32)
             )
@@ -74,10 +73,8 @@ def tile_picked_yhpspc_gate_p_kernel(
             grouped = keep.tile([P, H * PACK], BF16, name=f"w1_grouped{g}", align_bytes=64)
             dst = grouped[:].rearrange("p (t m r j) -> p m j r t", t=PACK, r=2, j=PACK)
             src = w1_raw[g][:].rearrange("p j (m r t) -> p m j r t", r=2, t=PACK)
-            if g == 0:
-                nc.scalar.copy(out=dst, in_=src)
-            else:
-                nc.vector.tensor_copy(out=dst, in_=src)
+            nc.vector.tensor_copy(out=dst[:, :40], in_=src[:, :40])
+            nc.scalar.copy(out=dst[:, 40:], in_=src[:, 40:])
             codes = keep.tile([P, H], U32, name=f"w1_codes{g}", align_bytes=64)
             scales = keep.tile([P, H], U8, name=f"w1_scales{g}", align_bytes=64)
             nc.vector.quantize_mx(out=codes[:].bitcast(FP8X4), scales=scales[:], in_=grouped[:])
@@ -88,7 +85,7 @@ def tile_picked_yhpspc_gate_p_kernel(
         nc.vector.tensor_copy(xs_picked[:], xs_all[:].indirect(offs_sb[:]))
         y_banks = [psum.tile([P, S], F32, name=f"y{t}") for t in range(PACK)]
         for g in range(PASSES):
-            x_picked = keep.tile([P, S], U32, name=f"x_picked{g}", align_bytes=64)
+            x_picked = keep.tile([P, S], U32, name="x_picked", align_bytes=64)
             nc.vector.tensor_copy(x_picked[:], x_all[g][:].bitcast(U32).indirect(offs_sb[:]))
             for t in range(PACK):
                 cols = slice(t * P, (t + 1) * P)
@@ -102,9 +99,8 @@ def tile_picked_yhpspc_gate_p_kernel(
                     stop=(g == PASSES - 1),
                 )
 
-        second = keep.tile([P, PACK, S], F32, name="second")
+        fetched = keep.tile([P, PACK, S], F32, name="fetched")
         second0 = keep.tile([P, S], F32, name="second0")
-        third = keep.tile([P, PACK, S], F32, name="third")
         prod = keep.tile([P, PACK, S], F32, name="prod")
         shifted = keep.tile([P, PACK, S], F32, name="shifted")
         root = keep.tile([P, PACK, S], F32, name="root")
@@ -112,24 +108,36 @@ def tile_picked_yhpspc_gate_p_kernel(
 
         for t in range(PACK):
             nc.scalar.activation(mag[t][:, :S], y_banks[t][:], ACT.Abs, scale=THIRD)
+        second = [second0[:]] + [fetched[:, t, :] for t in range(1, PACK)]
         for t in range(PACK):
             if t == 0:
-                nc.vector.tensor_copy(second0[:], mag[t][:].indirect(h2_sb[:]))
-                nc.vector.tensor_scalar_add(second[:, t, :], second0[:], FLOOR)
+                nc.vector.tensor_copy(fetched[:, t, :], mag[t][:].indirect(h2_sb[:]))
+                nc.vector.tensor_scalar_add(second[t], fetched[:, t, :], FLOOR)
             else:
-                nc.scalar.activation(
-                    second[:, t, :], mag[t][:].indirect(h2_sb[:]), ACT.Copy, bias=FLOOR
-                )
-        for t in range(PACK):
+                nc.scalar.activation(second[t], mag[t][:].indirect(h2_sb[:]), ACT.Copy, bias=FLOOR)
+
+        def product(t):
             nc.vector.scalar_tensor_tensor(
-                prod[:, t, :], second[:, t, :], FLOOR, mag[t][:, :S], ALU.subtract, ALU.mult
+                prod[:, t, :], second[t], FLOOR, mag[t][:, :S], ALU.subtract, ALU.mult
             )
             nc.scalar.activation(
                 root[:, t, :], prod[:, t, :], ACT.Sqrt, bias=0.05, scale=1.0 / THIRD**2
             )
+
+        def shifted_product(t):
             nc.vector.scalar_tensor_tensor(
-                shifted[:, t, :], mag[t][:, :S], FLOOR, second[:, t, :], ALU.add, ALU.mult
+                shifted[:, t, :], mag[t][:, :S], FLOOR, second[t], ALU.add, ALU.mult
             )
+
+        product(0)
+        shifted_product(0)
+        product(1)
+        shifted_product(1)
+        product(2)
+        product(3)
+        shifted_product(2)
+        shifted_product(3)
+        third = fetched
         for t in range(PACK):
             nc.vector.tensor_copy(third[:, t, :], mag[t][:].indirect(h3_sb[:]))
         log12 = prod
@@ -167,7 +175,8 @@ def tile_picked_yhpspc_gate_p_kernel(
                     ALU.mult, ALU.mult,
                 )
             hid_grouped = keep.tile([P, CHUNK * PACK], BF16, name=f"hid_grouped{c}", align_bytes=64)
-            nc.vector.tensor_copy(
+            weave = nc.scalar.copy if c in (1, 2) else nc.vector.tensor_copy
+            weave(
                 out=hid_grouped[:].rearrange("p (c i t) -> p c t i", i=4, t=PACK),
                 in_=hid[:].rearrange("p t (c i) -> p c t i", i=4),
             )

@@ -20,6 +20,9 @@ PACK = 4
 K_PASS = P * PACK
 PASSES = K // K_PASS
 WINDOW = 704
+WIDE_WINDOW = 2048
+ON_VECTOR = 2
+HALF = S // 2
 CHUNK = 128
 CHUNKS = S // CHUNK
 THIRD = 0.4
@@ -42,26 +45,31 @@ def tile_picked_yhpspc_gate_p_kernel(
         xs_all = keep.tile([P, T], U8, name="xs_all")
         w2_raw = keep.tile([P, PACK, N], F32, name="w2_raw")
         unit_sb = keep.tile([P, PACK], F32, name="unit_sb")
-        mag = [keep.tile([P, WINDOW], F32, name=f"mag{t}") for t in range(PACK)]
+        mag = [
+            keep.tile([P, WIDE_WINDOW if t < ON_VECTOR else WINDOW], F32, name=f"mag{t}")
+            for t in range(PACK)
+        ]
 
-        nc.gpsimd.memset(xs_all[:].bitcast(I32), 0)
-        for q in range(4):
-            nc.gpsimd.dma_start(
-                out=xs_all[32 * q : 32 * q + 4 * PASSES, :].bitcast(I32),
-                in_=x_scales[:, 4 * q : 4 * q + 4, :].bitcast(I32),
-            )
+        nc.vector.memset(xs_all[:].bitcast(I32), 0)
         for t in range(PACK):
             nc.vector.memset(mag[t][:, S:], 0.0)
         warm = keep.tile([P, 1], F32, name="warm")
         nc.scalar.activation(warm[:], mag[0][:, S : S + 1], ACT.Sqrt, bias=0.05)
 
+        w1_rows = w1.rearrange("(g p j) c -> g p j c", p=P, j=PACK)
+        x_rows = [x_words[g].rearrange("p n t -> p (n t)").bitcast(I32) for g in range(PASSES)]
         nc.sync.dma_start(offs_sb[:], offs)
-        for g in range(PASSES):
-            rows = w1[g * K_PASS : (g + 1) * K_PASS, :].rearrange("(p j) c -> p j c", j=PACK)
-            nc.sync.dma_start(out=w1_raw[g][:], in_=rows)
+        for j in range(PACK):
+            nc.sync.dma_start(out=w1_raw[0][:, j, :], in_=w1_rows[0][:, j, :])
+        for lo, hi in ((0, 768), (768, 1536), (1536, T)):
+            nc.sync.dma_start(out=x_all[0][:, lo:hi], in_=x_rows[0][:, lo:hi])
+        for q in range(4):
             nc.sync.dma_start(
-                out=x_all[g][:], in_=x_words[g].rearrange("p n t -> p (n t)").bitcast(I32)
+                out=xs_all[32 * q : 32 * q + 4 * PASSES, :].bitcast(I32),
+                in_=x_scales[:, 4 * q : 4 * q + 4, :].bitcast(I32),
             )
+        nc.sync.dma_start(out=w1_raw[1][:], in_=w1_rows[1])
+        nc.sync.dma_start(out=x_all[1][:], in_=x_rows[1])
         nc.sync.dma_start(h2_sb[:], h2)
         nc.sync.dma_start(h3_sb[:], h3)
         nc.sync.dma_start(out=w2_raw[:], in_=w2.rearrange("(p j) c -> p j c", j=PACK))
@@ -83,36 +91,48 @@ def tile_picked_yhpspc_gate_p_kernel(
 
         xs_picked = keep.tile([P, S], U8, name="xs_picked", align_bytes=64)
         nc.vector.tensor_copy(xs_picked[:], xs_all[:].indirect(offs_sb[:]))
-        y_banks = [psum.tile([P, S], F32, name=f"y{t}") for t in range(PACK)]
+        y_banks = [
+            [psum.tile([P, HALF], F32, name=f"bank{t}{h}") for h in range(2)] for t in range(PACK)
+        ]
         for g in range(PASSES):
-            x_picked = keep.tile([P, S], U32, name="x_picked", align_bytes=64)
-            nc.vector.tensor_copy(x_picked[:], x_all[g][:].bitcast(U32).indirect(offs_sb[:]))
+            x_picked = keep.tile([P, S], U32, name=f"x_picked{g}", align_bytes=64)
+            for h in range(2):
+                picks = slice(h * HALF, (h + 1) * HALF)
+                nc.vector.tensor_copy(
+                    x_picked[:, picks],
+                    x_all[g][:].bitcast(U32).indirect(offs_sb[:, h * HALF // 16 : (h + 1) * HALF // 16]),
+                )
             for t in range(PACK):
                 cols = slice(t * P, (t + 1) * P)
-                nc.tensor.matmul_mx(
-                    out=y_banks[t][:],
-                    lhsT=w1_codes[g][:, cols].bitcast(FP8X4),
-                    lhsT_scale=w1_scales[g][:, cols],
-                    rhs=x_picked[:].bitcast(FP8X4),
-                    rhs_scale=xs_picked[4 * g :, :],
-                    start=(g == 0),
-                    stop=(g == PASSES - 1),
-                )
+                for h in range(2):
+                    picks = slice(h * HALF, (h + 1) * HALF)
+                    nc.tensor.matmul_mx(
+                        out=y_banks[t][h][:],
+                        lhsT=w1_codes[g][:, cols].bitcast(FP8X4),
+                        lhsT_scale=w1_scales[g][:, cols],
+                        rhs=x_picked[:, picks].bitcast(FP8X4),
+                        rhs_scale=xs_picked[4 * g :, picks],
+                        start=(g == 0),
+                        stop=(g == PASSES - 1),
+                    )
 
         fetched = keep.tile([P, PACK, S], F32, name="fetched")
-        second0 = keep.tile([P, S], F32, name="second0")
         prod = keep.tile([P, PACK, S], F32, name="prod")
         shifted = keep.tile([P, PACK, S], F32, name="shifted")
         root = keep.tile([P, PACK, S], F32, name="root")
         hps = keep.tile([P, PACK, S], F32, name="hps")
 
         for t in range(PACK):
-            nc.scalar.activation(mag[t][:, :S], y_banks[t][:], ACT.Abs, scale=THIRD)
-        second = [second0[:]] + [fetched[:, t, :] for t in range(1, PACK)]
+            for h in range(2):
+                nc.scalar.activation(
+                    mag[t][:, h * HALF : (h + 1) * HALF], y_banks[t][h][:], ACT.Abs, scale=THIRD
+                )
+        second = [fetched[:, t, :] for t in range(PACK)]
         for t in range(PACK):
-            if t == 0:
-                nc.vector.tensor_copy(fetched[:, t, :], mag[t][:].indirect(h2_sb[:]))
-                nc.vector.tensor_scalar_add(second[t], fetched[:, t, :], FLOOR)
+            if t < ON_VECTOR:
+                nc.vector.tensor_scalar(
+                    second[t], mag[t][:].indirect(h2_sb[:]), 1.0, FLOOR, ALU.mult, ALU.add
+                )
             else:
                 nc.scalar.activation(second[t], mag[t][:].indirect(h2_sb[:]), ACT.Copy, bias=FLOOR)
 
@@ -129,33 +149,35 @@ def tile_picked_yhpspc_gate_p_kernel(
                 shifted[:, t, :], mag[t][:, :S], FLOOR, second[t], ALU.add, ALU.mult
             )
 
-        product(0)
-        shifted_product(0)
-        product(1)
-        shifted_product(1)
-        product(2)
-        product(3)
-        shifted_product(2)
-        shifted_product(3)
+        for t in range(PACK):
+            product(t)
+        for t in range(PACK):
+            shifted_product(t)
         third = fetched
         for t in range(PACK):
             nc.vector.tensor_copy(third[:, t, :], mag[t][:].indirect(h3_sb[:]))
-        log12 = prod
-        nc.scalar.activation(log12[:], shifted[:], ACT.Ln, scale=1.0 / THIRD**2)
+        log12 = [prod[:, (t + 2) % PACK, :] for t in range(PACK)]
+        for lo in (0, 2):
+            to = (lo + 2) % PACK
+            nc.scalar.activation(
+                prod[:, to : to + 2, :], shifted[:, lo : lo + 2, :], ACT.Ln, scale=1.0 / THIRD**2
+            )
         log3 = shifted
         for t in range(PACK):
             nc.scalar.activation(log3[:, t, :], third[:, t, :], ACT.Ln, bias=0.2, scale=1.0 / THIRD)
         for t in range(PACK):
-            nc.vector.tensor_tensor(root[:, t, :], third[:, t, :], root[:, t, :], ALU.subtract)
+            engine = nc.gpsimd if t < PACK - 1 else nc.vector
+            engine.tensor_tensor(root[:, t, :], third[:, t, :], root[:, t, :], ALU.subtract)
         for t in range(PACK):
             nc.vector.scalar_tensor_tensor(
-                hps[:, t, :], log3[:, t, :], 0.7, log12[:, t, :], ALU.mult, ALU.add
+                hps[:, t, :], log3[:, t, :], 0.7, log12[t], ALU.mult, ALU.add
             )
 
         w2_grouped = keep.tile([P, N * PACK], BF16, name="w2_grouped", align_bytes=64)
-        nc.vector.tensor_copy(
-            out=w2_grouped[:].rearrange("p (c i j) -> p c j i", i=4, j=PACK),
-            in_=w2_raw[:].rearrange("p j (c i) -> p c j i", i=4),
+        nc.gpsimd.tensor_scalar(
+            w2_grouped[:].rearrange("p (c j) -> p c j", j=PACK),
+            w2_raw[:].rearrange("p j c -> p c j"),
+            1.0, 0.0, ALU.mult, ALU.add,
         )
         w2_codes = keep.tile([P, N], U32, name="w2_codes", align_bytes=64)
         w2_scales = keep.tile([P, N], U8, name="w2_scales", align_bytes=64)
@@ -166,26 +188,34 @@ def tile_picked_yhpspc_gate_p_kernel(
             cols = slice(c * CHUNK, (c + 1) * CHUNK)
             nc.scalar.activation(gate[:, :, cols], root[:, :, cols], ACT.Sigmoid, scale=-1.0)
         out_rows = out.rearrange("(h p) j -> p h j", p=P)
-        for c in range(CHUNKS):
+        hid = [keep.tile([P, PACK, CHUNK], BF16, name=f"hid{c}") for c in range(CHUNKS)]
+        hid_grouped = [
+            keep.tile([P, CHUNK * PACK], BF16, name=f"hid_grouped{c}", align_bytes=64)
+            for c in range(CHUNKS)
+        ]
+
+        def gated(c):
             cols = slice(c * CHUNK, (c + 1) * CHUNK)
-            hid = keep.tile([P, PACK, CHUNK], BF16, name=f"hid{c}")
             for t in range(PACK):
                 nc.vector.scalar_tensor_tensor(
-                    hid[:, t, :], hps[:, t, cols], unit_sb[:, t : t + 1], gate[:, t, cols],
+                    hid[c][:, t, :], hps[:, t, cols], unit_sb[:, t : t + 1], gate[:, t, cols],
                     ALU.mult, ALU.mult,
                 )
-            hid_grouped = keep.tile([P, CHUNK * PACK], BF16, name=f"hid_grouped{c}", align_bytes=64)
-            weave = nc.scalar.copy if c in (1, 2) else nc.vector.tensor_copy
-            weave(
-                out=hid_grouped[:].rearrange("p (c i t) -> p c t i", i=4, t=PACK),
-                in_=hid[:].rearrange("p t (c i) -> p c t i", i=4),
+
+        def interleave(c):
+            nc.vector.tensor_copy(
+                out=hid_grouped[c][:].rearrange("p (c i t) -> p c t i", i=4, t=PACK),
+                in_=hid[c][:].rearrange("p t (c i) -> p c t i", i=4),
             )
+
+        def second_product(c):
+            cols = slice(c * CHUNK, (c + 1) * CHUNK)
             hid_codes = keep.tile([P, CHUNK], U32, name=f"hid_codes{c}", align_bytes=64)
             hid_scales = keep.tile([P, CHUNK], U8, name=f"hid_scales{c}", align_bytes=64)
             nc.vector.quantize_mx(
-                out=hid_codes[:].bitcast(FP8X4), scales=hid_scales[:], in_=hid_grouped[:]
+                out=hid_codes[:].bitcast(FP8X4), scales=hid_scales[:], in_=hid_grouped[c][:]
             )
-            acc = psum.tile([P, N // P, CHUNK], F32, name=f"acc{c}")
+            acc = psum.tile([P, N // P, CHUNK], F32, name=f"bank{c}0")
             for h in range(N // P):
                 rows = slice(h * P, (h + 1) * P)
                 nc.tensor.matmul_mx(
@@ -200,3 +230,11 @@ def tile_picked_yhpspc_gate_p_kernel(
             result = keep.tile([P, N // P, CHUNK], F32, name=f"result{c}")
             nc.scalar.copy(out=result[:], in_=acc[:])
             nc.sync.dma_start(out=out_rows[:, :, cols], in_=result[:])
+
+        for step in range(CHUNKS + 2):
+            if step < CHUNKS:
+                gated(step)
+            if 0 <= step - 2:
+                second_product(step - 2)
+            if 0 <= step - 1 < CHUNKS:
+                interleave(step - 1)

@@ -20,8 +20,7 @@ PACK = 4
 K_PASS = P * PACK
 PASSES = K // K_PASS
 WINDOW = 704
-WIDE_WINDOW = 2048
-ON_VECTOR = 2
+ON_VECTOR = 1
 HALF = S // 2
 CHUNK = 128
 CHUNKS = S // CHUNK
@@ -46,7 +45,7 @@ def tile_picked_yhpspc_gate_p_kernel(
         w2_raw = keep.tile([P, PACK, N], F32, name="w2_raw")
         unit_sb = keep.tile([P, PACK], F32, name="unit_sb")
         mag = [
-            keep.tile([P, WIDE_WINDOW if t < ON_VECTOR else WINDOW], F32, name=f"mag{t}")
+            keep.tile([P, WINDOW], F32, name=f"mag{t}")
             for t in range(PACK)
         ]
 
@@ -59,8 +58,10 @@ def tile_picked_yhpspc_gate_p_kernel(
         w1_rows = w1.rearrange("(g p j) c -> g p j c", p=P, j=PACK)
         x_rows = [x_words[g].rearrange("p n t -> p (n t)").bitcast(I32) for g in range(PASSES)]
         nc.sync.dma_start(offs_sb[:], offs)
-        for j in range(PACK):
-            nc.sync.dma_start(out=w1_raw[0][:, j, :], in_=w1_rows[0][:, j, :])
+        nc.sync.dma_start(h2_sb[:], h2)
+        nc.sync.dma_start(h3_sb[:], h3)
+        for j in (0, 2):
+            nc.sync.dma_start(out=w1_raw[0][:, j : j + 2, :], in_=w1_rows[0][:, j : j + 2, :])
         for lo, hi in ((0, 768), (768, 1536), (1536, T)):
             nc.sync.dma_start(out=x_all[0][:, lo:hi], in_=x_rows[0][:, lo:hi])
         for q in range(4):
@@ -70,8 +71,6 @@ def tile_picked_yhpspc_gate_p_kernel(
             )
         nc.sync.dma_start(out=w1_raw[1][:], in_=w1_rows[1])
         nc.sync.dma_start(out=x_all[1][:], in_=x_rows[1])
-        nc.sync.dma_start(h2_sb[:], h2)
-        nc.sync.dma_start(h3_sb[:], h3)
         nc.sync.dma_start(out=w2_raw[:], in_=w2.rearrange("(p j) c -> p j c", j=PACK))
         nc.sync.dma_start(out=unit_sb[:], in_=unit.rearrange("(p t) o -> p (t o)", t=PACK))
 
@@ -127,12 +126,12 @@ def tile_picked_yhpspc_gate_p_kernel(
                 nc.scalar.activation(
                     mag[t][:, h * HALF : (h + 1) * HALF], y_banks[t][h][:], ACT.Abs, scale=THIRD
                 )
-        second = [fetched[:, t, :] for t in range(PACK)]
+        second0 = keep.tile([P, S], F32, name="second0")
+        second = [second0[:]] + [fetched[:, t, :] for t in range(1, PACK)]
         for t in range(PACK):
             if t < ON_VECTOR:
-                nc.vector.tensor_scalar(
-                    second[t], mag[t][:].indirect(h2_sb[:]), 1.0, FLOOR, ALU.mult, ALU.add
-                )
+                nc.vector.tensor_copy(fetched[:, t, :], mag[t][:].indirect(h2_sb[:]))
+                nc.vector.tensor_scalar_add(second[t], fetched[:, t, :], FLOOR)
             else:
                 nc.scalar.activation(second[t], mag[t][:].indirect(h2_sb[:]), ACT.Copy, bias=FLOOR)
 
@@ -151,7 +150,6 @@ def tile_picked_yhpspc_gate_p_kernel(
 
         for t in range(PACK):
             product(t)
-        for t in range(PACK):
             shifted_product(t)
         third = fetched
         for t in range(PACK):
@@ -166,18 +164,16 @@ def tile_picked_yhpspc_gate_p_kernel(
         for t in range(PACK):
             nc.scalar.activation(log3[:, t, :], third[:, t, :], ACT.Ln, bias=0.2, scale=1.0 / THIRD)
         for t in range(PACK):
-            engine = nc.gpsimd if t < PACK - 1 else nc.vector
-            engine.tensor_tensor(root[:, t, :], third[:, t, :], root[:, t, :], ALU.subtract)
+            nc.vector.tensor_tensor(root[:, t, :], third[:, t, :], root[:, t, :], ALU.subtract)
         for t in range(PACK):
             nc.vector.scalar_tensor_tensor(
                 hps[:, t, :], log3[:, t, :], 0.7, log12[t], ALU.mult, ALU.add
             )
 
         w2_grouped = keep.tile([P, N * PACK], BF16, name="w2_grouped", align_bytes=64)
-        nc.gpsimd.tensor_scalar(
-            w2_grouped[:].rearrange("p (c j) -> p c j", j=PACK),
-            w2_raw[:].rearrange("p j c -> p c j"),
-            1.0, 0.0, ALU.mult, ALU.add,
+        nc.vector.tensor_copy(
+            out=w2_grouped[:].rearrange("p (c i j) -> p c j i", i=4, j=PACK),
+            in_=w2_raw[:].rearrange("p j (c i) -> p c j i", i=4),
         )
         w2_codes = keep.tile([P, N], U32, name="w2_codes", align_bytes=64)
         w2_scales = keep.tile([P, N], U8, name="w2_scales", align_bytes=64)
@@ -203,7 +199,8 @@ def tile_picked_yhpspc_gate_p_kernel(
                 )
 
         def interleave(c):
-            nc.vector.tensor_copy(
+            weave = nc.scalar.copy if c < 2 else nc.vector.tensor_copy
+            weave(
                 out=hid_grouped[c][:].rearrange("p (c i t) -> p c t i", i=4, t=PACK),
                 in_=hid[c][:].rearrange("p t (c i) -> p c t i", i=4),
             )
@@ -231,10 +228,12 @@ def tile_picked_yhpspc_gate_p_kernel(
             nc.scalar.copy(out=result[:], in_=acc[:])
             nc.sync.dma_start(out=out_rows[:, :, cols], in_=result[:])
 
-        for step in range(CHUNKS + 2):
-            if step < CHUNKS:
-                gated(step)
-            if 0 <= step - 2:
-                second_product(step - 2)
-            if 0 <= step - 1 < CHUNKS:
-                interleave(step - 1)
+        for c in range(CHUNKS):
+            gated(c)
+        interleave(0)
+        interleave(1)
+        interleave(2)
+        second_product(0)
+        interleave(3)
+        for c in range(1, CHUNKS):
+            second_product(c)

@@ -17,15 +17,28 @@ ALU = mybir.AluOpType
 
 P = 128
 PACK = 4
-K_PASS = P * PACK
-PASSES = K // K_PASS
-WINDOW = 704
-ON_VECTOR = 1
+PASSES = K // (P * PACK)
+LIST_ROWS = 16
+QUADRANT = 32
+SCALE_ROWS = 4
 HALF = S // 2
 CHUNK = 128
 CHUNKS = S // CHUNK
-THIRD = 0.4
-FLOOR = 0.2 * THIRD
+
+WINDOW = 704
+WIDE_WINDOW = 2048
+
+H2_ON_VECTOR = 2
+W1_ON_VECTOR = 84
+HID_ON_SCALAR = 2
+
+X_FIRST_CUTS = (0, 768, 1536, T)
+
+TABLE_SCALE = 0.4
+LOG_FLOOR = 0.2
+ROOT_FLOOR = 0.05
+THIRD_WEIGHT = 0.7
+SHIFT = LOG_FLOOR * TABLE_SCALE
 
 
 def tile_picked_yhpspc_gate_p_kernel(
@@ -36,38 +49,38 @@ def tile_picked_yhpspc_gate_p_kernel(
         keep = ctx.enter_context(tc.tile_pool(name="keep", bufs=1))
         psum = ctx.enter_context(tc.psum_pool(name="psum", bufs=1))
 
-        offs_sb = keep.tile([P, S // 16], U16, name="offs_sb")
-        h2_sb = keep.tile([P, S // 16], U16, name="h2_sb")
-        h3_sb = keep.tile([P, S // 16], U16, name="h3_sb")
+        offs_sb = keep.tile([P, S // LIST_ROWS], U16, name="offs_sb")
+        h2_sb = keep.tile([P, S // LIST_ROWS], U16, name="h2_sb")
+        h3_sb = keep.tile([P, S // LIST_ROWS], U16, name="h3_sb")
         w1_raw = [keep.tile([P, PACK, H], F32, name=f"w1_raw{g}") for g in range(PASSES)]
         x_all = [keep.tile([P, T], I32, name=f"x_all{g}") for g in range(PASSES)]
         xs_all = keep.tile([P, T], U8, name="xs_all")
         w2_raw = keep.tile([P, PACK, N], F32, name="w2_raw")
         unit_sb = keep.tile([P, PACK], F32, name="unit_sb")
-        mag = [
-            keep.tile([P, WINDOW], F32, name=f"mag{t}")
+        table = [
+            keep.tile([P, WIDE_WINDOW if t < H2_ON_VECTOR else WINDOW], F32, name=f"table{t}")
             for t in range(PACK)
         ]
 
         nc.vector.memset(xs_all[:].bitcast(I32), 0)
         for t in range(PACK):
-            nc.vector.memset(mag[t][:, S:], 0.0)
+            nc.vector.memset(table[t][:, S:], 0.0)
         warm = keep.tile([P, 1], F32, name="warm")
-        nc.scalar.activation(warm[:], mag[0][:, S : S + 1], ACT.Sqrt, bias=0.05)
+        nc.scalar.activation(warm[:], table[0][:, S : S + 1], ACT.Sqrt, bias=ROOT_FLOOR)
 
         w1_rows = w1.rearrange("(g p j) c -> g p j c", p=P, j=PACK)
-        x_rows = [x_words[g].rearrange("p n t -> p (n t)").bitcast(I32) for g in range(PASSES)]
+        x_rows = [x_words[g].rearrange("p n j -> p (n j)").bitcast(I32) for g in range(PASSES)]
         nc.sync.dma_start(offs_sb[:], offs)
         nc.sync.dma_start(h2_sb[:], h2)
         nc.sync.dma_start(h3_sb[:], h3)
-        for j in (0, 2):
+        for j in range(0, PACK, 2):
             nc.sync.dma_start(out=w1_raw[0][:, j : j + 2, :], in_=w1_rows[0][:, j : j + 2, :])
-        for lo, hi in ((0, 768), (768, 1536), (1536, T)):
+        for lo, hi in zip(X_FIRST_CUTS, X_FIRST_CUTS[1:]):
             nc.sync.dma_start(out=x_all[0][:, lo:hi], in_=x_rows[0][:, lo:hi])
-        for q in range(4):
+        for q in range(P // QUADRANT):
             nc.sync.dma_start(
-                out=xs_all[32 * q : 32 * q + 4 * PASSES, :].bitcast(I32),
-                in_=x_scales[:, 4 * q : 4 * q + 4, :].bitcast(I32),
+                out=xs_all[QUADRANT * q : QUADRANT * q + SCALE_ROWS * PASSES, :].bitcast(I32),
+                in_=x_scales[:, SCALE_ROWS * q : SCALE_ROWS * (q + 1), :].bitcast(I32),
             )
         nc.sync.dma_start(out=w1_raw[1][:], in_=w1_rows[1])
         nc.sync.dma_start(out=x_all[1][:], in_=x_rows[1])
@@ -78,15 +91,21 @@ def tile_picked_yhpspc_gate_p_kernel(
         w1_scales = []
         for g in range(PASSES):
             grouped = keep.tile([P, H * PACK], BF16, name=f"w1_grouped{g}", align_bytes=64)
-            dst = grouped[:].rearrange("p (t m r j) -> p m j r t", t=PACK, r=2, j=PACK)
-            src = w1_raw[g][:].rearrange("p j (m r t) -> p m j r t", r=2, t=PACK)
-            nc.vector.tensor_copy(out=dst[:, :40], in_=src[:, :40])
-            nc.scalar.copy(out=dst[:, 40:], in_=src[:, 40:])
+            dst = grouped[:].rearrange("p (t m j) -> p m t j", t=PACK, j=PACK)
+            src = w1_raw[g][:].rearrange("p j (m t) -> p m t j", t=PACK)
+            nc.vector.tensor_copy(out=dst[:, :W1_ON_VECTOR], in_=src[:, :W1_ON_VECTOR])
+            nc.scalar.copy(out=dst[:, W1_ON_VECTOR:], in_=src[:, W1_ON_VECTOR:])
             codes = keep.tile([P, H], U32, name=f"w1_codes{g}", align_bytes=64)
             scales = keep.tile([P, H], U8, name=f"w1_scales{g}", align_bytes=64)
             nc.vector.quantize_mx(out=codes[:].bitcast(FP8X4), scales=scales[:], in_=grouped[:])
             w1_codes.append(codes)
             w1_scales.append(scales)
+
+        def half(h):
+            return slice(h * HALF, (h + 1) * HALF)
+
+        def half_list(h):
+            return slice(h * HALF // LIST_ROWS, (h + 1) * HALF // LIST_ROWS)
 
         xs_picked = keep.tile([P, S], U8, name="xs_picked", align_bytes=64)
         nc.vector.tensor_copy(xs_picked[:], xs_all[:].indirect(offs_sb[:]))
@@ -96,78 +115,84 @@ def tile_picked_yhpspc_gate_p_kernel(
         for g in range(PASSES):
             x_picked = keep.tile([P, S], U32, name=f"x_picked{g}", align_bytes=64)
             for h in range(2):
-                picks = slice(h * HALF, (h + 1) * HALF)
                 nc.vector.tensor_copy(
-                    x_picked[:, picks],
-                    x_all[g][:].bitcast(U32).indirect(offs_sb[:, h * HALF // 16 : (h + 1) * HALF // 16]),
+                    x_picked[:, half(h)],
+                    x_all[g][:].bitcast(U32).indirect(offs_sb[:, half_list(h)]),
                 )
             for t in range(PACK):
-                cols = slice(t * P, (t + 1) * P)
+                features = slice(t * P, (t + 1) * P)
                 for h in range(2):
-                    picks = slice(h * HALF, (h + 1) * HALF)
                     nc.tensor.matmul_mx(
                         out=y_banks[t][h][:],
-                        lhsT=w1_codes[g][:, cols].bitcast(FP8X4),
-                        lhsT_scale=w1_scales[g][:, cols],
-                        rhs=x_picked[:, picks].bitcast(FP8X4),
-                        rhs_scale=xs_picked[4 * g :, picks],
+                        lhsT=w1_codes[g][:, features].bitcast(FP8X4),
+                        lhsT_scale=w1_scales[g][:, features],
+                        rhs=x_picked[:, half(h)].bitcast(FP8X4),
+                        rhs_scale=xs_picked[SCALE_ROWS * g :, half(h)],
                         start=(g == 0),
                         stop=(g == PASSES - 1),
                     )
 
-        fetched = keep.tile([P, PACK, S], F32, name="fetched")
-        prod = keep.tile([P, PACK, S], F32, name="prod")
-        shifted = keep.tile([P, PACK, S], F32, name="shifted")
-        root = keep.tile([P, PACK, S], F32, name="root")
+        buf_fetch = keep.tile([P, PACK, S], F32, name="buf_fetch")
+        buf_prod = keep.tile([P, PACK, S], F32, name="buf_prod")
+        buf_shift = keep.tile([P, PACK, S], F32, name="buf_shift")
+        buf_root = keep.tile([P, PACK, S], F32, name="buf_root")
         hps = keep.tile([P, PACK, S], F32, name="hps")
 
         for t in range(PACK):
             for h in range(2):
                 nc.scalar.activation(
-                    mag[t][:, h * HALF : (h + 1) * HALF], y_banks[t][h][:], ACT.Abs, scale=THIRD
+                    table[t][:, half(h)], y_banks[t][h][:], ACT.Abs, scale=TABLE_SCALE
                 )
-        second0 = keep.tile([P, S], F32, name="second0")
-        second = [second0[:]] + [fetched[:, t, :] for t in range(1, PACK)]
+
+        second = buf_fetch
         for t in range(PACK):
-            if t < ON_VECTOR:
-                nc.vector.tensor_copy(fetched[:, t, :], mag[t][:].indirect(h2_sb[:]))
-                nc.vector.tensor_scalar_add(second[t], fetched[:, t, :], FLOOR)
+            looked_up = table[t][:].indirect(h2_sb[:])
+            if t < H2_ON_VECTOR:
+                nc.vector.tensor_scalar(second[:, t, :], looked_up, 1.0, SHIFT, ALU.mult, ALU.add)
             else:
-                nc.scalar.activation(second[t], mag[t][:].indirect(h2_sb[:]), ACT.Copy, bias=FLOOR)
+                nc.scalar.activation(second[:, t, :], looked_up, ACT.Copy, bias=SHIFT)
 
-        def product(t):
+        prod, shifted, root = buf_prod, buf_shift, buf_root
+        for t in range(PACK):
+            m = table[t][:, :S]
             nc.vector.scalar_tensor_tensor(
-                prod[:, t, :], second[t], FLOOR, mag[t][:, :S], ALU.subtract, ALU.mult
+                prod[:, t, :], second[:, t, :], SHIFT, m, ALU.subtract, ALU.mult
             )
             nc.scalar.activation(
-                root[:, t, :], prod[:, t, :], ACT.Sqrt, bias=0.05, scale=1.0 / THIRD**2
+                root[:, t, :], prod[:, t, :], ACT.Sqrt, bias=ROOT_FLOOR, scale=1.0 / TABLE_SCALE**2
             )
-
-        def shifted_product(t):
             nc.vector.scalar_tensor_tensor(
-                shifted[:, t, :], mag[t][:, :S], FLOOR, second[t], ALU.add, ALU.mult
+                shifted[:, t, :], m, SHIFT, second[:, t, :], ALU.add, ALU.mult
             )
 
-        for t in range(PACK):
-            product(t)
-            shifted_product(t)
-        third = fetched
-        for t in range(PACK):
-            nc.vector.tensor_copy(third[:, t, :], mag[t][:].indirect(h3_sb[:]))
-        log12 = [prod[:, (t + 2) % PACK, :] for t in range(PACK)]
-        for lo in (0, 2):
-            to = (lo + 2) % PACK
+        third = buf_fetch
+        nc.scalar.activation(
+            third[:, 0, half(0)], table[0][:].indirect(h3_sb[:, half_list(0)]), ACT.Copy
+        )
+        nc.vector.tensor_copy(third[:, 0, half(1)], table[0][:].indirect(h3_sb[:, half_list(1)]))
+        for t in range(1, PACK):
+            nc.vector.tensor_copy(third[:, t, :], table[t][:].indirect(h3_sb[:]))
+
+        log12 = [buf_prod[:, (t + 2) % PACK, :] for t in range(PACK)]
+        for t in range(0, PACK, 2):
+            to = (t + 2) % PACK
             nc.scalar.activation(
-                prod[:, to : to + 2, :], shifted[:, lo : lo + 2, :], ACT.Ln, scale=1.0 / THIRD**2
+                buf_prod[:, to : to + 2, :],
+                shifted[:, t : t + 2, :],
+                ACT.Ln,
+                scale=1.0 / TABLE_SCALE**2,
             )
-        log3 = shifted
+        log3 = buf_shift
         for t in range(PACK):
-            nc.scalar.activation(log3[:, t, :], third[:, t, :], ACT.Ln, bias=0.2, scale=1.0 / THIRD)
+            nc.scalar.activation(
+                log3[:, t, :], third[:, t, :], ACT.Ln, bias=LOG_FLOOR, scale=1.0 / TABLE_SCALE
+            )
+        minus_sal = buf_root
         for t in range(PACK):
-            nc.vector.tensor_tensor(root[:, t, :], third[:, t, :], root[:, t, :], ALU.subtract)
+            nc.vector.tensor_tensor(minus_sal[:, t, :], third[:, t, :], root[:, t, :], ALU.subtract)
         for t in range(PACK):
             nc.vector.scalar_tensor_tensor(
-                hps[:, t, :], log3[:, t, :], 0.7, log12[t], ALU.mult, ALU.add
+                hps[:, t, :], log3[:, t, :], THIRD_WEIGHT, log12[t], ALU.mult, ALU.add
             )
 
         w2_grouped = keep.tile([P, N * PACK], BF16, name="w2_grouped", align_bytes=64)
@@ -179,11 +204,16 @@ def tile_picked_yhpspc_gate_p_kernel(
         w2_scales = keep.tile([P, N], U8, name="w2_scales", align_bytes=64)
         nc.vector.quantize_mx(out=w2_codes[:].bitcast(FP8X4), scales=w2_scales[:], in_=w2_grouped[:])
 
-        gate = third
+        def chunk(c):
+            return slice(c * CHUNK, (c + 1) * CHUNK)
+
+        gate = buf_fetch
         for c in range(CHUNKS):
-            cols = slice(c * CHUNK, (c + 1) * CHUNK)
-            nc.scalar.activation(gate[:, :, cols], root[:, :, cols], ACT.Sigmoid, scale=-1.0)
-        out_rows = out.rearrange("(h p) j -> p h j", p=P)
+            nc.scalar.activation(
+                gate[:, :, chunk(c)], minus_sal[:, :, chunk(c)], ACT.Sigmoid, scale=-1.0
+            )
+
+        out_rows = out.rearrange("(r p) j -> p r j", p=P)
         hid = [keep.tile([P, PACK, CHUNK], BF16, name=f"hid{c}") for c in range(CHUNKS)]
         hid_grouped = [
             keep.tile([P, CHUNK * PACK], BF16, name=f"hid_grouped{c}", align_bytes=64)
@@ -191,34 +221,36 @@ def tile_picked_yhpspc_gate_p_kernel(
         ]
 
         def gated(c):
-            cols = slice(c * CHUNK, (c + 1) * CHUNK)
             for t in range(PACK):
                 nc.vector.scalar_tensor_tensor(
-                    hid[c][:, t, :], hps[:, t, cols], unit_sb[:, t : t + 1], gate[:, t, cols],
-                    ALU.mult, ALU.mult,
+                    hid[c][:, t, :],
+                    hps[:, t, chunk(c)],
+                    unit_sb[:, t : t + 1],
+                    gate[:, t, chunk(c)],
+                    ALU.mult,
+                    ALU.mult,
                 )
 
         def interleave(c):
-            weave = nc.scalar.copy if c < 2 else nc.vector.tensor_copy
-            weave(
-                out=hid_grouped[c][:].rearrange("p (c i t) -> p c t i", i=4, t=PACK),
-                in_=hid[c][:].rearrange("p t (c i) -> p c t i", i=4),
+            move = nc.scalar.copy if c < HID_ON_SCALAR else nc.vector.tensor_copy
+            move(
+                out=hid_grouped[c][:].rearrange("p (b i t) -> p b t i", i=4, t=PACK),
+                in_=hid[c][:].rearrange("p t (b i) -> p b t i", i=4),
             )
 
         def second_product(c):
-            cols = slice(c * CHUNK, (c + 1) * CHUNK)
             hid_codes = keep.tile([P, CHUNK], U32, name=f"hid_codes{c}", align_bytes=64)
             hid_scales = keep.tile([P, CHUNK], U8, name=f"hid_scales{c}", align_bytes=64)
             nc.vector.quantize_mx(
                 out=hid_codes[:].bitcast(FP8X4), scales=hid_scales[:], in_=hid_grouped[c][:]
             )
             acc = psum.tile([P, N // P, CHUNK], F32, name=f"bank{c}0")
-            for h in range(N // P):
-                rows = slice(h * P, (h + 1) * P)
+            for r in range(N // P):
+                pitches = slice(r * P, (r + 1) * P)
                 nc.tensor.matmul_mx(
-                    out=acc[:, h, :],
-                    lhsT=w2_codes[:, rows].bitcast(FP8X4),
-                    lhsT_scale=w2_scales[:, rows],
+                    out=acc[:, r, :],
+                    lhsT=w2_codes[:, pitches].bitcast(FP8X4),
+                    lhsT_scale=w2_scales[:, pitches],
                     rhs=hid_codes[:].bitcast(FP8X4),
                     rhs_scale=hid_scales[:],
                     start=True,
@@ -226,14 +258,13 @@ def tile_picked_yhpspc_gate_p_kernel(
                 )
             result = keep.tile([P, N // P, CHUNK], F32, name=f"result{c}")
             nc.scalar.copy(out=result[:], in_=acc[:])
-            nc.sync.dma_start(out=out_rows[:, :, cols], in_=result[:])
+            nc.sync.dma_start(out=out_rows[:, :, chunk(c)], in_=result[:])
 
         for c in range(CHUNKS):
             gated(c)
-        interleave(0)
-        interleave(1)
-        interleave(2)
+        for c in range(CHUNKS - 1):
+            interleave(c)
         second_product(0)
-        interleave(3)
+        interleave(CHUNKS - 1)
         for c in range(1, CHUNKS):
             second_product(c)

from contextlib import ExitStack

import concourse.mybir as mybir

K, T, S, N, H = 1024, 2048, 512, 256, 512
FLOPS = 2 * K * H * S + 2 * H * N * S

F32 = mybir.dt.float32
BF16 = mybir.dt.bfloat16
I32 = mybir.dt.int32
U32 = mybir.dt.uint32
U16 = mybir.dt.uint16
U8 = mybir.dt.uint8
FP8X4 = mybir.dt.float8_e4m3fn_x4
ACT = mybir.ActivationFunctionType
ALU = mybir.AluOpType

P = 128
PACK = 4
PASSES = K // (P * PACK)
LIST_ROWS = 16
QUADRANT = 32
SCALE_ROWS = 4
HALF = S // 2
CHUNK = 128
CHUNKS = S // CHUNK

WINDOW = 704
WIDE_WINDOW = 2048

H2_ON_VECTOR = 2
W1_ON_VECTOR = 84
HID_ON_SCALAR = 2

X_FIRST_CUTS = (0, 768, 1536, T)

TABLE_SCALE = 0.4
LOG_FLOOR = 0.2
ROOT_FLOOR = 0.05
THIRD_WEIGHT = 0.7
SHIFT = LOG_FLOOR * TABLE_SCALE


def tile_picked_yhpspc_gate_p_kernel(
    tc, x_words, x_scales, w1, unit, w2, offs, h2, h3, out
):
    nc = tc.nc
    with ExitStack() as ctx:
        keep = ctx.enter_context(tc.tile_pool(name="keep", bufs=1))
        psum = ctx.enter_context(tc.psum_pool(name="psum", bufs=1))

        offs_sb = keep.tile([P, S // LIST_ROWS], U16, name="offs_sb")
        h2_sb = keep.tile([P, S // LIST_ROWS], U16, name="h2_sb")
        h3_sb = keep.tile([P, S // LIST_ROWS], U16, name="h3_sb")
        w1_raw = [keep.tile([P, PACK, H], F32, name=f"w1_raw{g}") for g in range(PASSES)]
        x_all = [keep.tile([P, T], I32, name=f"x_all{g}") for g in range(PASSES)]
        xs_all = keep.tile([P, T], U8, name="xs_all")
        w2_raw = keep.tile([P, PACK, N], F32, name="w2_raw")
        unit_sb = keep.tile([P, PACK], F32, name="unit_sb")
        table = [
            keep.tile([P, WIDE_WINDOW if t < H2_ON_VECTOR else WINDOW], F32, name=f"table{t}")
            for t in range(PACK)
        ]

        nc.vector.memset(xs_all[:].bitcast(I32), 0)
        for t in range(PACK):
            nc.vector.memset(table[t][:, S:], 0.0)
        warm = keep.tile([P, 1], F32, name="warm")
        nc.scalar.activation(warm[:], table[0][:, S : S + 1], ACT.Sqrt, bias=ROOT_FLOOR)

        w1_rows = w1.rearrange("(g p j) c -> g p j c", p=P, j=PACK)
        x_rows = [x_words[g].rearrange("p n j -> p (n j)").bitcast(I32) for g in range(PASSES)]
        nc.sync.dma_start(offs_sb[:], offs)
        nc.sync.dma_start(h2_sb[:], h2)
        nc.sync.dma_start(h3_sb[:], h3)
        for j in range(0, PACK, 2):
            nc.sync.dma_start(out=w1_raw[0][:, j : j + 2, :], in_=w1_rows[0][:, j : j + 2, :])
        for lo, hi in zip(X_FIRST_CUTS, X_FIRST_CUTS[1:]):
            nc.sync.dma_start(out=x_all[0][:, lo:hi], in_=x_rows[0][:, lo:hi])
        for q in range(P // QUADRANT):
            nc.sync.dma_start(
                out=xs_all[QUADRANT * q : QUADRANT * q + SCALE_ROWS * PASSES, :].bitcast(I32),
                in_=x_scales[:, SCALE_ROWS * q : SCALE_ROWS * (q + 1), :].bitcast(I32),
            )
        nc.sync.dma_start(out=w1_raw[1][:], in_=w1_rows[1])
        nc.sync.dma_start(out=x_all[1][:], in_=x_rows[1])
        nc.sync.dma_start(out=w2_raw[:], in_=w2.rearrange("(p j) c -> p j c", j=PACK))
        nc.sync.dma_start(out=unit_sb[:], in_=unit.rearrange("(p t) o -> p (t o)", t=PACK))

        w1_codes = []
        w1_scales = []
        for g in range(PASSES):
            grouped = keep.tile([P, H * PACK], BF16, name=f"w1_grouped{g}", align_bytes=64)
            dst = grouped[:].rearrange("p (t m j) -> p m t j", t=PACK, j=PACK)
            src = w1_raw[g][:].rearrange("p j (m t) -> p m t j", t=PACK)
            nc.vector.tensor_copy(out=dst[:, :W1_ON_VECTOR], in_=src[:, :W1_ON_VECTOR])
            nc.scalar.copy(out=dst[:, W1_ON_VECTOR:], in_=src[:, W1_ON_VECTOR:])
            codes = keep.tile([P, H], U32, name=f"w1_codes{g}", align_bytes=64)
            scales = keep.tile([P, H], U8, name=f"w1_scales{g}", align_bytes=64)
            nc.vector.quantize_mx(out=codes[:].bitcast(FP8X4), scales=scales[:], in_=grouped[:])
            w1_codes.append(codes)
            w1_scales.append(scales)

        def half(h):
            return slice(h * HALF, (h + 1) * HALF)

        def half_list(h):
            return slice(h * HALF // LIST_ROWS, (h + 1) * HALF // LIST_ROWS)

        xs_picked = keep.tile([P, S], U8, name="xs_picked", align_bytes=64)
        nc.vector.tensor_copy(xs_picked[:], xs_all[:].indirect(offs_sb[:]))
        y_banks = [
            [psum.tile([P, HALF], F32, name=f"bank{t}{h}") for h in range(2)] for t in range(PACK)
        ]
        for g in range(PASSES):
            x_picked = keep.tile([P, S], U32, name=f"x_picked{g}", align_bytes=64)
            for h in range(2):
                nc.vector.tensor_copy(
                    x_picked[:, half(h)],
                    x_all[g][:].bitcast(U32).indirect(offs_sb[:, half_list(h)]),
                )
            for t in range(PACK):
                features = slice(t * P, (t + 1) * P)
                for h in range(2):
                    nc.tensor.matmul_mx(
                        out=y_banks[t][h][:],
                        lhsT=w1_codes[g][:, features].bitcast(FP8X4),
                        lhsT_scale=w1_scales[g][:, features],
                        rhs=x_picked[:, half(h)].bitcast(FP8X4),
                        rhs_scale=xs_picked[SCALE_ROWS * g :, half(h)],
                        start=(g == 0),
                        stop=(g == PASSES - 1),
                    )

        buf_fetch = keep.tile([P, PACK, S], F32, name="buf_fetch")
        buf_prod = keep.tile([P, PACK, S], F32, name="buf_prod")
        buf_shift = keep.tile([P, PACK, S], F32, name="buf_shift")
        buf_root = keep.tile([P, PACK, S], F32, name="buf_root")
        hps = keep.tile([P, PACK, S], F32, name="hps")

        for t in range(PACK):
            for h in range(2):
                nc.scalar.activation(
                    table[t][:, half(h)], y_banks[t][h][:], ACT.Abs, scale=TABLE_SCALE
                )

        second = buf_fetch
        for t in range(PACK):
            looked_up = table[t][:].indirect(h2_sb[:])
            if t < H2_ON_VECTOR:
                nc.vector.tensor_scalar(second[:, t, :], looked_up, 1.0, SHIFT, ALU.mult, ALU.add)
            else:
                nc.scalar.activation(second[:, t, :], looked_up, ACT.Copy, bias=SHIFT)

        prod, shifted, root = buf_prod, buf_shift, buf_root
        for t in range(PACK):
            m = table[t][:, :S]
            nc.vector.scalar_tensor_tensor(
                prod[:, t, :], second[:, t, :], SHIFT, m, ALU.subtract, ALU.mult
            )
            nc.scalar.activation(
                root[:, t, :], prod[:, t, :], ACT.Sqrt, bias=ROOT_FLOOR, scale=1.0 / TABLE_SCALE**2
            )
            nc.vector.scalar_tensor_tensor(
                shifted[:, t, :], m, SHIFT, second[:, t, :], ALU.add, ALU.mult
            )

        third = buf_fetch
        nc.scalar.activation(
            third[:, 0, half(0)], table[0][:].indirect(h3_sb[:, half_list(0)]), ACT.Copy
        )
        nc.vector.tensor_copy(third[:, 0, half(1)], table[0][:].indirect(h3_sb[:, half_list(1)]))
        for t in range(1, PACK):
            nc.vector.tensor_copy(third[:, t, :], table[t][:].indirect(h3_sb[:]))

        log12 = [buf_prod[:, (t + 2) % PACK, :] for t in range(PACK)]
        for t in range(0, PACK, 2):
            to = (t + 2) % PACK
            nc.scalar.activation(
                buf_prod[:, to : to + 2, :],
                shifted[:, t : t + 2, :],
                ACT.Ln,
                scale=1.0 / TABLE_SCALE**2,
            )
        log3 = buf_shift
        for t in range(PACK):
            nc.scalar.activation(
                log3[:, t, :], third[:, t, :], ACT.Ln, bias=LOG_FLOOR, scale=1.0 / TABLE_SCALE
            )
        minus_sal = buf_root
        for t in range(PACK):
            nc.vector.tensor_tensor(minus_sal[:, t, :], third[:, t, :], root[:, t, :], ALU.subtract)
        for t in range(PACK):
            nc.vector.scalar_tensor_tensor(
                hps[:, t, :], log3[:, t, :], THIRD_WEIGHT, log12[t], ALU.mult, ALU.add
            )

        w2_grouped = keep.tile([P, N * PACK], BF16, name="w2_grouped", align_bytes=64)
        nc.vector.tensor_copy(
            out=w2_grouped[:].rearrange("p (c i j) -> p c j i", i=4, j=PACK),
            in_=w2_raw[:].rearrange("p j (c i) -> p c j i", i=4),
        )
        w2_codes = keep.tile([P, N], U32, name="w2_codes", align_bytes=64)
        w2_scales = keep.tile([P, N], U8, name="w2_scales", align_bytes=64)
        nc.vector.quantize_mx(out=w2_codes[:].bitcast(FP8X4), scales=w2_scales[:], in_=w2_grouped[:])

        def chunk(c):
            return slice(c * CHUNK, (c + 1) * CHUNK)

        gate = buf_fetch
        for c in range(CHUNKS):
            nc.scalar.activation(
                gate[:, :, chunk(c)], minus_sal[:, :, chunk(c)], ACT.Sigmoid, scale=-1.0
            )

        out_rows = out.rearrange("(r p) j -> p r j", p=P)
        hid = [keep.tile([P, PACK, CHUNK], BF16, name=f"hid{c}") for c in range(CHUNKS)]
        hid_grouped = [
            keep.tile([P, CHUNK * PACK], BF16, name=f"hid_grouped{c}", align_bytes=64)
            for c in range(CHUNKS)
        ]

        def gated(c):
            for t in range(PACK):
                nc.vector.scalar_tensor_tensor(
                    hid[c][:, t, :],
                    hps[:, t, chunk(c)],
                    unit_sb[:, t : t + 1],
                    gate[:, t, chunk(c)],
                    ALU.mult,
                    ALU.mult,
                )

        def interleave(c):
            move = nc.scalar.copy if c < HID_ON_SCALAR else nc.vector.tensor_copy
            move(
                out=hid_grouped[c][:].rearrange("p (b i t) -> p b t i", i=4, t=PACK),
                in_=hid[c][:].rearrange("p t (b i) -> p b t i", i=4),
            )

        def second_product(c):
            hid_codes = keep.tile([P, CHUNK], U32, name=f"hid_codes{c}", align_bytes=64)
            hid_scales = keep.tile([P, CHUNK], U8, name=f"hid_scales{c}", align_bytes=64)
            nc.vector.quantize_mx(
                out=hid_codes[:].bitcast(FP8X4), scales=hid_scales[:], in_=hid_grouped[c][:]
            )
            acc = psum.tile([P, N // P, CHUNK], F32, name=f"bank{c}0")
            for r in range(N // P):
                pitches = slice(r * P, (r + 1) * P)
                nc.tensor.matmul_mx(
                    out=acc[:, r, :],
                    lhsT=w2_codes[:, pitches].bitcast(FP8X4),
                    lhsT_scale=w2_scales[:, pitches],
                    rhs=hid_codes[:].bitcast(FP8X4),
                    rhs_scale=hid_scales[:],
                    start=True,
                    stop=True,
                )
            result = keep.tile([P, N // P, CHUNK], F32, name=f"result{c}")
            nc.scalar.copy(out=result[:], in_=acc[:])
            nc.sync.dma_start(out=out_rows[:, :, chunk(c)], in_=result[:])

        for c in range(CHUNKS):
            gated(c)
        for c in range(CHUNKS - 1):
            interleave(c)
        second_product(0)
        interleave(CHUNKS - 1)
        for c in range(1, CHUNKS):
            second_product(c)
